import numpy as np
import ml_dtypes


def mxq(x, axis, fmt="e4m3"):
    dtype, down = {"e4m3": (ml_dtypes.float8_e4m3fn, 7), "e5m2": (ml_dtypes.float8_e5m2, 14)}[fmt]
    v = np.moveaxis(np.asarray(x, np.float32).astype(ml_dtypes.bfloat16).astype(np.float64), axis, -1)
    blocks = v.reshape(v.shape[:-1] + (-1, 32))
    amax = np.abs(blocks).max(-1, keepdims=True)
    byte = np.maximum(np.where(amax > 0, np.frexp(amax)[1] - 1 + 127, 0) - down, 1)
    scale = np.exp2(byte - 127.0)
    codes = (blocks / scale).astype(np.float32).astype(dtype).astype(np.float64)
    return np.moveaxis((codes * scale).reshape(v.shape), -1, axis)


WIDE = False


def mx_kscale(k):
    if not WIDE:
        return np.ones(k)
    levels = np.array([10, -10, 5, -5, 0])
    if k % 512:
        return np.exp2(np.random.permutation(np.resize(levels, k // 32))).repeat(32)
    a = np.empty((k // 512, 16))
    for p in range(k // 512):
        a[p, :8] = np.random.permutation(np.resize(levels, 8))
        for g in range(8):
            far = levels[np.abs(levels - a[p, g]) >= 10]
            a[p, g + 8] = far[np.random.randint(len(far))]
    return np.exp2(a.ravel()).repeat(32)


BF16 = ml_dtypes.bfloat16


def bf(x):
    return np.asarray(x, np.float32).astype(BF16)


def f64(x):
    return np.asarray(x).astype(np.float64)


E2M1 = np.array([0.0, 0.5, 1.0, 1.5, 2.0, 3.0, 4.0, 6.0, -0.0, -0.5, -1.0, -1.5, -2.0, -3.0, -4.0, -6.0])


def pack_weight(w, fmt):
    k, n = w.shape
    w = f64(bf(w)).reshape(k // 32, 32, n)
    amax = np.abs(w).max(1)
    if fmt == "e4m3":
        byte = np.frexp(amax)[1] - 1 + 127 - 7
    else:
        mant, ex = np.frexp(amax / 6.0)
        byte = np.where(mant > 0.5, ex, ex - 1) + 127
    byte = np.clip(np.where(amax > 0, byte, 1), 1, 254)
    scaled = (w * np.exp2(127.0 - byte)[:, None, :]).reshape(k, n).astype(np.float32)
    by_word = np.ascontiguousarray(scaled.reshape(k // 512, 128, 4, n).transpose(0, 1, 3, 2))
    if fmt == "e4m3":
        words = by_word.astype(ml_dtypes.float8_e4m3fn).view(np.uint8)
    else:
        c = by_word.astype(ml_dtypes.float4_e2m1fn).view(np.uint8) & 0xF
        words = c[..., 0::2] | (c[..., 1::2] << 4)
    return np.ascontiguousarray(words), np.ascontiguousarray(byte.astype(np.uint8).reshape(k // 512, 16, n))


def unpack_weight(words, scales, fmt):
    g, p, n, _ = words.shape
    if fmt == "e4m3":
        vals = np.ascontiguousarray(words).view(ml_dtypes.float8_e4m3fn).astype(np.float64)
    else:
        nib = np.empty((g, p, n, 4), np.uint8)
        nib[..., 0::2] = words & 0xF
        nib[..., 1::2] = words >> 4
        vals = E2M1[nib]
    vals = vals * np.repeat(np.exp2(scales.astype(np.float64) - 127.0), 8, axis=1)[..., None]
    return vals.transpose(0, 1, 3, 2).reshape(g * 512, n)

def planes(Y):
    n, m = Y.shape
    b = f64(bf(Y)).reshape(n // 32, 32, m)
    amax = np.abs(b).max(1)
    byte = np.clip(np.where(amax > 0, np.frexp(amax)[1] - 1 + 127 - 7, 1), 1, 254)
    codes = (b * np.exp2(127.0 - byte)[:, None, :]).reshape(n, m).astype(np.float32).astype(ml_dtypes.float8_e4m3fn).view(np.uint8)
    words = codes.reshape(n // 512, 128, 4, m).transpose(0, 1, 3, 2)
    return np.ascontiguousarray(words), np.ascontiguousarray(byte.astype(np.uint8).reshape(n // 512, 16, m))


B, P, H, V, J, D, E = 128, 512, 1024, 2048, 512, 3, 4


def setup_inputs():
    s, t, r = mx_kscale(P), mx_kscale(H), mx_kscale(J)
    pose = bf(np.random.standard_normal((B, P)) * s)
    w1_words, w1_scales = pack_weight(np.random.standard_normal((P, H)) / np.sqrt(P) / s[:, None], "e4m3")
    g = bf((1.0 + 0.1 * np.random.standard_normal(H)) * t)
    basis = bf(np.random.standard_normal((H, V, D)) / np.sqrt(H) / t[:, None, None])
    template = bf(np.random.standard_normal((V, D)))
    skin_words, skin_scales = pack_weight((np.random.standard_normal((V, J)) / np.sqrt(J) * r).T, "e4m3")
    xf = bf(np.random.standard_normal((J, B, D, E)) / r[:, None, None, None])
    return {
        "pose": pose,
        "w1_words": w1_words,
        "w1_scales": w1_scales,
        "g": g,
        "basis": basis,
        "template": template,
        "skin_words": skin_words,
        "skin_scales": skin_scales,
        "xf": xf,
    }


def blend_coefficients(pose, w1_words, w1_scales, g):
    return np.tanh(mxq(f64(pose), 1, "e4m3") @ unpack_weight(w1_words, w1_scales, "e4m3")) * f64(g)[None, :]


def blended_transforms(skin_words, skin_scales, xf):
    xq = mxq(f64(xf).reshape(J, B * D * E), 0, "e4m3")
    sq = unpack_weight(skin_words, skin_scales, "e4m3").T
    return (xq.T @ sq.T).reshape(B, D, E, V).transpose(0, 3, 1, 2)


def core(pose, w1_words, w1_scales, g, basis, template, skin_words, skin_scales, xf):
    coef = blend_coefficients(pose, w1_words, w1_scales, g)
    off = (mxq(coef, 1, "e4m3") @ mxq(f64(basis).reshape(H, V * D), 0, "e4m3")).reshape(B, V, D)
    u = f64(template)[None, :, :] + off
    m = blended_transforms(skin_words, skin_scales, xf)
    linear = m[..., :D]
    translation = m[..., D]
    return np.sum(linear * u[:, :, None, :], axis=-1) + translation


def reference(pose, w1_words, w1_scales, g, basis, template, skin_words, skin_scales, xf):
    R_out = core(pose, w1_words, w1_scales, g, basis, template, skin_words, skin_scales, xf)
    words, scales = planes(np.moveaxis(R_out, 1, 0).reshape(2048, -1))
    return R_out, words, scales

@@ -1,0 +1,349 @@
+from contextlib import ExitStack
+
+import concourse.mybir as mybir
+from concourse.masks import make_identity
+
+B, PD, H, V, J = 128, 512, 1024, 2048, 512
+FLOPS = 2 * B * PD * H + 2 * B * H * V * 3 + 2 * B * 12 * J * V
+
+F32 = mybir.dt.float32
+BF16 = mybir.dt.bfloat16
+U32 = mybir.dt.uint32
+I32 = mybir.dt.int32
+U8 = mybir.dt.uint8
+FP8X4 = mybir.dt.float8_e4m3fn_x4
+ACT = mybir.ActivationFunctionType
+ALU = mybir.AluOpType
+
+P = 128
+TILES = V // P
+CHUNK = 2
+SCALAR_N = 96
+
+
+def tile_neuralblendshapelinearskinning_x2_kernel(
+    tc, pose, w1_words, w1_scales, g, basis, template, skin_words, skin_scales, xf, out_0, out_1, out_2
+):
+    nc = tc.nc
+    with ExitStack() as ctx:
+        keep = ctx.enter_context(tc.tile_pool(name="keep", bufs=1))
+        work = ctx.enter_context(tc.tile_pool(name="work", bufs=2))
+        psum = ctx.enter_context(tc.psum_pool(name="psum", bufs=1))
+        ctx.enter_context(tc.manual_schedule())
+
+        def bank(tag, shape, dtype=F32):
+            return psum.tile(shape, dtype, tag=tag, name=tag)
+
+        def copy_on(engine, out, in_):
+            if engine == "vector":
+                nc.vector.tensor_copy(out=out, in_=in_)
+            else:
+                nc.scalar.copy(out=out, in_=in_)
+
+        def quantize(codes, scales, values, spans):
+            for lo, hi in spans:
+                nc.vector.quantize_mx(
+                    out=codes[:, lo:hi].bitcast(FP8X4), scales=scales[:, lo:hi], in_=values[:, 4 * lo : 4 * hi]
+                )
+
+        def mx(out, lhs, lhs_cols, rhs, rhs_cols, start=True, stop=True):
+            nc.tensor.matmul_mx(
+                out=out,
+                lhsT=lhs[0][:, lhs_cols].bitcast(FP8X4),
+                lhsT_scale=lhs[1][:, lhs_cols],
+                rhs=rhs[0][:, rhs_cols].bitcast(FP8X4),
+                rhs_scale=rhs[1][:, rhs_cols],
+                start=start,
+                stop=stop,
+            )
+
+        w1_c = keep.tile([P, H], U32, align_bytes=64)
+        w1_s = keep.tile([P, H], U8, align_bytes=64)
+        skin_c = keep.tile([P, V], U32, align_bytes=64)
+        skin_s = keep.tile([P, V], U8, align_bytes=64)
+        tmpl_rows = keep.tile([P, 3 * P], BF16)
+        zero = keep.tile([P, 1], F32)
+        zero_bias = keep.tile([P, 1], F32)
+        nc.vector.memset(zero[:], 0.0)
+        nc.vector.memset(w1_s[:].bitcast(I32), 0)
+        nc.vector.memset(tmpl_rows[:], 0.0)
+        nc.vector.memset(skin_s[:].bitcast(I32), 0)
+        nc.scalar.activation(out=zero_bias[:], in_=zero[:], func=ACT.Tanh)
+        ident = keep.tile([P, P], F32)
+        ident_bf = keep.tile([P, P], BF16)
+        make_identity(nc, ident[:])
+        make_identity(nc, ident_bf[:])
+
+        pose_sb = keep.tile([P, PD], BF16)
+        xf_rows = xf.rearrange("(p t) b i k -> p t (b i k)", t=4)
+        xf_raw = [keep.tile([P, 4, 768], BF16, name="xf_raw%d" % h) for h in range(2)]
+        gain = keep.tile([P, 2, 4], BF16)
+        basis_rows = basis.rearrange("(g p t) n c -> g p t (n c)", g=2, t=4)
+        raw = {}
+
+        def load_scales(queue, plane, rows):
+            for quad in range(4):
+                queue.dma_start(
+                    out=plane[32 * quad : 32 * quad + 4, :].bitcast(I32),
+                    in_=rows[0, 4 * quad : 4 * quad + 4, :].bitcast(I32),
+                )
+
+        def load_words(codes, words, lo, hi):
+            nc.sync.dma_start(
+                out=codes[:, lo:hi].bitcast(I32),
+                in_=words[0].rearrange("p n t -> p (n t)")[:, 4 * lo : 4 * hi].bitcast(I32),
+            )
+
+        def load_basis(chunk):
+            first = CHUNK * chunk
+            count = CHUNK
+            for half in range(2):
+                rows = keep.tile([P, 4, 384 * count], BF16, name="basis_raw%d_%d" % (chunk, half))
+                nc.sync.dma_start(out=rows[:], in_=basis_rows[half, :, :, 384 * first : 384 * (first + count)])
+                for q in range(count):
+                    raw[first + q, half] = rows[:, :, 384 * q : 384 * (q + 1)]
+
+        nc.sync.dma_start(out=pose_sb[:], in_=pose)
+        nc.sync.dma_start(out=xf_raw[0][:], in_=xf_rows[:, :, 0:768])
+        nc.sync.dma_start(out=xf_raw[1][:], in_=xf_rows[:, :, 768:1536])
+        load_words(w1_c, w1_words, 0, H)
+        load_scales(nc.sync, w1_s, w1_scales)
+        nc.gpsimd.dma_start(out=gain[:], in_=g.rearrange("(g p t) -> p g t", g=2, t=4))
+        nc.gpsimd.dma_start(out=tmpl_rows[0:TILES, :], in_=template.rearrange("(q n) c -> q (n c)", n=P))
+        load_scales(nc.gpsimd, skin_s, skin_scales)
+        load_basis(0)
+        load_words(skin_c, skin_words, 0, 512)
+        load_basis(1)
+        load_words(skin_c, skin_words, 512, V)
+        load_basis(2)
+
+        pose_words = pose_sb[:].bitcast(F32)
+        pose_t = bank("wa", [P, 2, P])
+        for u in range(2):
+            nc.tensor.transpose(pose_t[:, u, :], pose_words[:, u : 256 : 2], ident[:])
+        pose_k = keep.tile([P, 4 * B], BF16, align_bytes=64)
+        nc.scalar.copy(
+            out=pose_k[:].bitcast(F32).rearrange("p (b u) -> p b u", u=2), in_=pose_t[:].rearrange("p u b -> p b u")
+        )
+        pose_q = (keep.tile([P, B], U32, align_bytes=64, name="pose_c"), keep.tile([P, B], U8, align_bytes=64, name="pose_s"))
+        quantize(pose_q[0], pose_q[1], pose_k, [(0, B)])
+
+        xf_k = keep.tile([P, 12 * B * 4], BF16, align_bytes=64)
+        xf_k5 = xf_k[:].rearrange("p (i k b t) -> p i b t k", i=3, k=4, t=4)
+
+        def interleave_xf(half, i, engine):
+            src = xf_raw[half][:].rearrange("p t (b i k) -> p i b t k", i=3, k=4)
+            copy_on(engine, xf_k5[:, i, 64 * half : 64 * half + 64], src[:, i])
+
+        interleave_xf(0, 0, "vector")
+        interleave_xf(0, 2, "scalar")
+        interleave_xf(0, 1, "vector")
+        interleave_xf(1, 0, "vector")
+
+        interleave_xf(1, 2, "scalar")
+        interleave_xf(1, 1, "vector")
+        xf_q = (keep.tile([P, 12 * B], U32, align_bytes=64, name="xf_c"), keep.tile([P, 12 * B], U8, align_bytes=64, name="xf_s"))
+        quantize(xf_q[0], xf_q[1], xf_k, [(1024, 1536), (0, 1024)])
+
+        tanh_sb = keep.tile([P, 2, 4, P], F32)
+        for half in range(2):
+            pre = bank("v%d" % half, [P, 512])
+            mx(pre[:], pose_q, slice(0, B), (w1_c, w1_s), slice(512 * half, 512 * half + 512))
+            nc.scalar.activation(
+                out=tanh_sb[:, half], in_=pre[:].rearrange("b (p t) -> b t p", t=4), func=ACT.Tanh, bias=zero_bias[:]
+            )
+        tmpl_t = bank("wb", [P, 3, P], BF16)
+        for c in range(3):
+            nc.tensor.transpose(tmpl_t[:, c, :], tmpl_rows[:, c : 3 * P : 3], ident_bf[:])
+        tmpl = keep.tile([P, 3, TILES], F32)
+        nc.scalar.copy(out=tmpl[:], in_=tmpl_t[:, :, 0:TILES])
+
+        coef_k = keep.tile([P, 2, B, 4], BF16, align_bytes=64)
+        for half in range(2):
+            tanh_t = bank(("off", "m3")[half], [P, 4, B])
+            for t in range(4):
+                nc.tensor.transpose(tanh_t[:, t, :], tanh_sb[:, half, t, :], ident[:])
+            nc.vector.tensor_tensor(
+                out=coef_k[:, half],
+                in0=tanh_t[:].rearrange("p t b -> p b t"),
+                in1=gain[:, half, :].unsqueeze(1).to_broadcast([P, B, 4]),
+                op=ALU.mult,
+            )
+        coef_q = (keep.tile([P, 2 * B], U32, align_bytes=64, name="coef_c"), keep.tile([P, 2 * B], U8, align_bytes=64, name="coef_s"))
+        quantize(coef_q[0], coef_q[1], coef_k[:].rearrange("p g b t -> p (g b t)"), [(0, 2 * B)])
+
+        basis_k, basis_q, off_ps, m3_ps, m_ps, u_sb, m3_sb, prod_sb, y_ps, y_bf, word_ps = ({} for k in range(11))
+        skin_q = (skin_c, skin_s)
+
+        def interleave_basis(q, half, lo, hi, engine):
+            if q not in basis_k:
+                basis_k[q] = work.tile([P, 2 * 3 * P * 4], BF16, align_bytes=64, bufs=3, name="basis_k")
+            dst = basis_k[q][:].rearrange("p (g c m l t) -> p g m t l c", g=2, c=3, l=2, t=4)
+            src = raw[q, half].rearrange("p t (m l c) -> p m t l c", l=2, c=3)
+            copy_on(engine, dst[:, half, lo // 2 : hi // 2], src[:, lo // 2 : hi // 2])
+
+        def interleave_range(q, lo, hi, engine):
+            interleave_basis(q, lo // P, lo % P, (hi - 1) % P + 1, engine)
+
+        def interleave_scalar(q):
+            interleave_range(q, 2 * P - SCALAR_N // 2, 2 * P, "scalar")
+            interleave_range(q, 2 * P - SCALAR_N, 2 * P - SCALAR_N // 2, "scalar")
+
+        def interleave_vector(q, hi=2 * P - SCALAR_N):
+            if hi > P:
+                interleave_range(q, P, hi, "vector")
+            interleave_range(q, 0, min(hi, P), "vector")
+
+        def quantize_basis(q):
+            basis_q[q] = (
+                work.tile([P, 6 * P], U32, align_bytes=64, name="basis_c"),
+                work.tile([P, 6 * P], U8, align_bytes=64, name="basis_s"),
+            )
+            quantize(basis_q[q][0], basis_q[q][1], basis_k[q], [(512, 768), (0, 512)])
+
+        def matmul_offsets(q):
+            off_ps[q] = bank("off", [P, 3, B])
+            for c in range(3):
+                for half in range(2):
+                    col = P * (3 * half + c)
+                    mx(off_ps[q][:, c, :], basis_q[q], slice(col, col + P), coef_q, slice(B * half, B * half + B),
+                       start=half == 0, stop=half == 1)
+            m3_ps[q] = bank("m3", [P, 3, B])
+            for i in range(3):
+                mx(m3_ps[q][:, i, :], skin_q, slice(P * q, P * q + P), xf_q, slice(512 * i + 384, 512 * i + 512))
+
+        def matmul_linear(q, tags=("v0", "v1", "v2")):
+            for i in range(3):
+                m_ps[q, i] = bank(tags[i], [P, 3 * B])
+                mx(m_ps[q, i][:, 0:256], skin_q, slice(P * q, P * q + P), xf_q, slice(512 * i, 512 * i + 256))
+                mx(m_ps[q, i][:, 256:384], skin_q, slice(P * q, P * q + P), xf_q, slice(512 * i + 256, 512 * i + 384))
+
+        def shaped(q):
+            u_sb[q] = work.tile([P, 3, B], F32, name="u_sb")
+            for c in range(3):
+                nc.scalar.activation(
+                    out=u_sb[q][:, c, :], in_=off_ps[q][:, c, :], func=ACT.Identity, bias=tmpl[:, c, q : q + 1]
+                )
+            m3_sb[q] = work.tile([P, 3, B], F32, name="m3_sb")
+            nc.scalar.copy(out=m3_sb[q][:], in_=m3_ps[q][:])
+
+        def products(q):
+            prod_sb[q] = work.tile([P, 3, 3 * B], F32, name="prod_sb")
+            for i in range(3):
+                nc.vector.tensor_tensor(
+                    out=prod_sb[q][:, i, :], in0=m_ps[q, i][:], in1=u_sb[q][:].rearrange("p c b -> p (c b)"), op=ALU.mult
+                )
+
+        def accumulate(q):
+            y_ps[q] = bank("off" if q == TILES - 1 else "y", [P, 3, P])
+            for i in range(3):
+                terms = [prod_sb[q][:, i, B * c : B * c + B] for c in range(3)] + [m3_sb[q][:, i, :]]
+                for k in range(4):
+                    nc.tensor.matmul(
+                        y_ps[q][:, i, :], lhsT=terms[k], rhs=ident[:], start=k == 0, stop=k == 3, is_transpose=True
+                    )
+
+        def round_out(q):
+            grp, r = divmod(q, 4)
+            if r == 0:
+                y_bf[grp] = work.tile([P, 3, 2, P, 2], BF16, name="y_bf")
+            nc.scalar.copy(
+                out=y_bf[grp][:, :, :, 32 * r : 32 * r + 32, :],
+                in_=y_ps[q][:].rearrange("b i (p u e) -> b i u p e", u=2, e=2),
+            )
+
+        def hand_out(q):
+            y_sb = work.tile([P, P, 3], F32, bufs=4)
+            nc.scalar.copy(out=y_sb[:], in_=y_ps[q][:].rearrange("b i n -> b n i"))
+            nc.sync.dma_start(out=out_0[:, P * q : P * q + P, :], in_=y_sb[:])
+
+        def turn_words(grp, tags=("wa", "wb")):
+            words = y_bf[grp][:].rearrange("b i u p e -> b (i u p e)").bitcast(F32)
+            low = bank(tags[0], [P, 8, 64])
+            high = bank(tags[1], [P, 8, 64])
+            word_ps[grp] = (low, high)
+            for j in range(6):
+                nc.tensor.transpose(low[:, j : 8 : 7 - j, :], words[:, P * j : P * j + P], ident[:])
+            for j in range(6):
+                nc.tensor.transpose(high[:, 0 : j + 2 : j + 1, :], words[:, P * j : P * j + P], ident[:])
+
+        plane_k = {}
+
+        def gather_words(grp):
+            plane_k[grp] = work.tile([P, 4 * 384], BF16, align_bytes=64, name="plane_k")
+            dst = plane_k[grp][:].bitcast(F32).rearrange("p (b j) -> p b j", j=6)
+            low, high = word_ps[grp]
+            nc.scalar.copy(out=dst[:, 0:64, :], in_=low[:, 0:6, :].rearrange("p j b -> p b j"))
+            copy_on("vector" if grp == 3 else "scalar", dst[:, 64:128, :], high[:, 1:7, :].rearrange("p j b -> p b j"))
+
+        def store_planes(grp):
+            plane_c = work.tile([P, 384], U32, align_bytes=64)
+            plane_s = work.tile([P, 384], U8, align_bytes=64)
+            quantize(plane_c, plane_s, plane_k[grp], [(0, 128), (128, 384)] if grp == 3 else [(0, 256), (256, 384)])
+            nc.sync.dma_start(
+                out=out_1[grp].rearrange("p m t -> p (m t)").bitcast(I32), in_=plane_c[:].bitcast(I32)
+            )
+            for quad in range(4):
+                nc.sync.dma_start(
+                    out=out_2[grp, 4 * quad : 4 * quad + 4, :].bitcast(I32),
+                    in_=plane_s[32 * quad : 32 * quad + 4, :].bitcast(I32),
+                )
+
+        def live(q):
+            return 0 <= q < TILES
+
+        interleave_range(0, 0, 64, "scalar")
+        interleave_range(0, 64, 128, "scalar")
+        interleave_range(1, 0, 128, "vector")
+        interleave_range(0, 192, 256, "scalar")
+        interleave_range(0, 128, 192, "vector")
+        interleave_range(1, 128, 160, "vector")
+        interleave_range(1, 160, 256, "scalar")
+        quantize_basis(0)
+        matmul_offsets(0)
+        shaped(0)
+        matmul_linear(0)
+        quantize_basis(1)
+        interleave_scalar(2)
+        last = TILES - 1
+        for s in range(last - 1):
+            matmul_offsets(s + 1)
+            products(s)
+            if s > 0:
+                round_out(s - 1)
+                hand_out(s - 1)
+            if s % 2 == 1 and live(s + 5):
+                load_basis(3 + s // 2)
+            if s + 2 == last:
+                interleave_range(last, 96, 128, "scalar")
+                interleave_range(last, 128, 160, "scalar")
+            shaped(s + 1)
+            matmul_linear(s + 1)
+            accumulate(s)
+            if s > 0 and s % 4 == 0:
+                turn_words(s // 4 - 1)
+            if s > 1 and s % 4 == 1:
+                gather_words(s // 4 - 1)
+            if live(s + 3):
+                interleave_scalar(s + 3)
+            interleave_vector(s + 2, 96 if s + 2 == last else 2 * P - SCALAR_N)
+            if s > 2 and s % 4 == 2:
+                store_planes(s // 4 - 1)
+            quantize_basis(s + 2)
+        matmul_offsets(last)
+        products(last - 1)
+        round_out(last - 2)
+        hand_out(last - 2)
+        shaped(last)
+        matmul_linear(last, ("wa", "wb", "v0"))
+        products(last)
+        store_planes(2)
+        accumulate(last - 1)
+        accumulate(last)
+        round_out(last - 1)
+        hand_out(last - 1)
+        round_out(last)
+        turn_words(3, ("v1", "v2"))
+        hand_out(last)
+        gather_words(3)
+        store_planes(3)

@@ -18,7 +18,7 @@ ALU = mybir.AluOpType
 P = 128
 TILES = V // P
 CHUNK = 2
-SCALAR_N = 96
+BLOCK = ((2, 3, 4), (0, 1, 5))
 
 
 def tile_neuralblendshapelinearskinning_x2_kernel(
@@ -81,9 +81,9 @@ def tile_neuralblendshapelinearskinning_x2_kernel(
         basis_rows = basis.rearrange("(g p t) n c -> g p t (n c)", g=2, t=4)
         raw = {}
 
-        def load_scales(queue, plane, rows):
+        def load_scales(plane, rows):
             for quad in range(4):
-                queue.dma_start(
+                nc.sync.dma_start(
                     out=plane[32 * quad : 32 * quad + 4, :].bitcast(I32),
                     in_=rows[0, 4 * quad : 4 * quad + 4, :].bitcast(I32),
                 )
@@ -94,10 +94,10 @@ def tile_neuralblendshapelinearskinning_x2_kernel(
                 in_=words[0].rearrange("p n t -> p (n t)")[:, 4 * lo : 4 * hi].bitcast(I32),
             )
 
-        def load_basis(chunk):
+        def load_basis(chunk, order=(1, 0)):
             first = CHUNK * chunk
             count = CHUNK
-            for half in range(2):
+            for half in order:
                 rows = keep.tile([P, 4, 384 * count], BF16, name="basis_raw%d_%d" % (chunk, half))
                 nc.sync.dma_start(out=rows[:], in_=basis_rows[half, :, :, 384 * first : 384 * (first + count)])
                 for q in range(count):
@@ -105,17 +105,19 @@ def tile_neuralblendshapelinearskinning_x2_kernel(
 
         nc.sync.dma_start(out=pose_sb[:], in_=pose)
         nc.sync.dma_start(out=xf_raw[0][:], in_=xf_rows[:, :, 0:768])
+        nc.sync.dma_start(out=gain[:], in_=g.rearrange("(g p t) -> p g t", g=2, t=4))
+        load_scales(w1_s, w1_scales)
+        nc.sync.dma_start(out=tmpl_rows[0:TILES, :], in_=template.rearrange("(q n) c -> q (n c)", n=P))
         nc.sync.dma_start(out=xf_raw[1][:], in_=xf_rows[:, :, 768:1536])
         load_words(w1_c, w1_words, 0, H)
-        load_scales(nc.sync, w1_s, w1_scales)
-        nc.gpsimd.dma_start(out=gain[:], in_=g.rearrange("(g p t) -> p g t", g=2, t=4))
-        nc.gpsimd.dma_start(out=tmpl_rows[0:TILES, :], in_=template.rearrange("(q n) c -> q (n c)", n=P))
-        load_scales(nc.gpsimd, skin_s, skin_scales)
-        load_basis(0)
-        load_words(skin_c, skin_words, 0, 512)
+        load_basis(0, (0, 1))
+        load_scales(skin_s, skin_scales)
+        load_words(skin_c, skin_words, 0, 256)
         load_basis(1)
-        load_words(skin_c, skin_words, 512, V)
+        load_words(skin_c, skin_words, 256, 768)
         load_basis(2)
+        load_words(skin_c, skin_words, 768, V)
+        load_basis(3)
 
         pose_words = pose_sb[:].bitcast(F32)
         pose_t = bank("wa", [P, 2, P])
@@ -175,37 +177,48 @@ def tile_neuralblendshapelinearskinning_x2_kernel(
         basis_k, basis_q, off_ps, m3_ps, m_ps, u_sb, m3_sb, prod_sb, y_ps, y_bf, word_ps = ({} for k in range(11))
         skin_q = (skin_c, skin_s)
 
-        def interleave_basis(q, half, lo, hi, engine):
-            if q not in basis_k:
-                basis_k[q] = work.tile([P, 2 * 3 * P * 4], BF16, align_bytes=64, bufs=3, name="basis_k")
-            dst = basis_k[q][:].rearrange("p (g c m l t) -> p g m t l c", g=2, c=3, l=2, t=4)
-            src = raw[q, half].rearrange("p t (m l c) -> p m t l c", l=2, c=3)
-            copy_on(engine, dst[:, half, lo // 2 : hi // 2], src[:, lo // 2 : hi // 2])
+        basis_g = {}
 
-        def interleave_range(q, lo, hi, engine):
-            interleave_basis(q, lo // P, lo % P, (hi - 1) % P + 1, engine)
+        def main_tile(q):
+            if q not in basis_k:
+                basis_k[q] = work.tile([P, 5 * P * 4], BF16, align_bytes=64, bufs=3, name="basis_k")
+            return basis_k[q]
+
+        def interleave_low(q, lo, hi, engine):
+            dst = main_tile(q)[:, 1024:2560].rearrange("p (c m l t) -> p m t l c", c=3, l=2, t=4)
+            src = raw[q, 0].rearrange("p t (m l c) -> p m t l c", l=2, c=3)
+            copy_on(engine, dst[:, lo // 2 : hi // 2], src[:, lo // 2 : hi // 2])
+
+        def interleave_high(q, lo, hi, engine):
+            dst = main_tile(q)[:, 0:1024].rearrange("p (c m l t) -> p m t l c", c=2, l=2, t=4)
+            src = raw[q, 1].rearrange("p t (m l c) -> p m t l c", l=2, c=3)
+            copy_on(engine, dst[:, lo // 2 : hi // 2], src[:, lo // 2 : hi // 2, :, :, 0:2])
+
+        def interleave_rest(q, engine):
+            basis_g[q] = keep.tile([P, P * 4], BF16, align_bytes=64, name="basis_first" if q == 0 else "basis_g")
+            dst = basis_g[q][:].rearrange("p (n t) -> p n t", t=4)
+            src = raw[q, 1].rearrange("p t (n c) -> p n t c", c=3)[:, :, :, 2]
+            if engine == "gpsimd":
+                nc.gpsimd.tensor_scalar(out=dst, in0=src, scalar1=1.0, scalar2=0.0, op0=ALU.mult, op1=ALU.add)
+            else:
+                copy_on(engine, dst, src)
 
         def interleave_scalar(q):
-            interleave_range(q, 2 * P - SCALAR_N // 2, 2 * P, "scalar")
-            interleave_range(q, 2 * P - SCALAR_N, 2 * P - SCALAR_N // 2, "scalar")
-
-        def interleave_vector(q, hi=2 * P - SCALAR_N):
-            if hi > P:
-                interleave_range(q, P, hi, "vector")
-            interleave_range(q, 0, min(hi, P), "vector")
+            interleave_high(q, 0, 64, "scalar")
+            interleave_high(q, 64, 128, "scalar")
 
         def quantize_basis(q):
-            basis_q[q] = (
-                work.tile([P, 6 * P], U32, align_bytes=64, name="basis_c"),
-                work.tile([P, 6 * P], U8, align_bytes=64, name="basis_s"),
-            )
-            quantize(basis_q[q][0], basis_q[q][1], basis_k[q], [(512, 768), (0, 512)])
+            codes = work.tile([P, 6 * P], U32, align_bytes=64, name="basis_c")
+            scales = work.tile([P, 6 * P], U8, align_bytes=64, name="basis_s")
+            basis_q[q] = (codes, scales)
+            quantize(codes, scales, basis_k[q], [(0, 256), (256, 512), (512, 640)])
+            quantize(codes[:, 640:768], scales[:, 640:768], basis_g[q], [(0, P)])
 
         def matmul_offsets(q):
             off_ps[q] = bank("off", [P, 3, B])
             for c in range(3):
                 for half in range(2):
-                    col = P * (3 * half + c)
+                    col = P * BLOCK[half][c]
                     mx(off_ps[q][:, c, :], basis_q[q], slice(col, col + P), coef_q, slice(B * half, B * half + B),
                        start=half == 0, stop=half == 1)
             m3_ps[q] = bank("m3", [P, 3, B])
@@ -292,13 +305,14 @@ def tile_neuralblendshapelinearskinning_x2_kernel(
         def live(q):
             return 0 <= q < TILES
 
-        interleave_range(0, 0, 64, "scalar")
-        interleave_range(0, 64, 128, "scalar")
-        interleave_range(1, 0, 128, "vector")
-        interleave_range(0, 192, 256, "scalar")
-        interleave_range(0, 128, 192, "vector")
-        interleave_range(1, 128, 160, "vector")
-        interleave_range(1, 160, 256, "scalar")
+        interleave_low(0, 0, 64, "scalar")
+        interleave_low(0, 64, 128, "scalar")
+        interleave_low(1, 0, 128, "vector")
+        interleave_high(0, 0, 64, "scalar")
+        interleave_high(0, 64, 128, "vector")
+        interleave_rest(0, "vector")
+        interleave_rest(1, "scalar")
+        interleave_scalar(1)
         quantize_basis(0)
         matmul_offsets(0)
         shaped(0)
@@ -308,15 +322,15 @@ def tile_neuralblendshapelinearskinning_x2_kernel(
         last = TILES - 1
         for s in range(last - 1):
             matmul_offsets(s + 1)
+            interleave_rest(s + 2, "gpsimd")
             products(s)
             if s > 0:
                 round_out(s - 1)
                 hand_out(s - 1)
-            if s % 2 == 1 and live(s + 5):
-                load_basis(3 + s // 2)
+            if s % 2 == 1 and live(s + 7):
+                load_basis(4 + s // 2)
             if s + 2 == last:
-                interleave_range(last, 96, 128, "scalar")
-                interleave_range(last, 128, 160, "scalar")
+                interleave_low(last, 96, 128, "scalar")
             shaped(s + 1)
             matmul_linear(s + 1)
             accumulate(s)
@@ -326,7 +340,7 @@ def tile_neuralblendshapelinearskinning_x2_kernel(
                 gather_words(s // 4 - 1)
             if live(s + 3):
                 interleave_scalar(s + 3)
-            interleave_vector(s + 2, 96 if s + 2 == last else 2 * P - SCALAR_N)
+            interleave_low(s + 2, 0, 96 if s + 2 == last else P, "vector")
             if s > 2 and s % 4 == 2:
                 store_planes(s // 4 - 1)
             quantize_basis(s + 2)

from contextlib import ExitStack

import concourse.mybir as mybir
from concourse.masks import make_identity

B, PD, H, V, J = 128, 512, 1024, 2048, 512
FLOPS = 2 * B * PD * H + 2 * B * H * V * 3 + 2 * B * 12 * J * V

F32 = mybir.dt.float32
BF16 = mybir.dt.bfloat16
U32 = mybir.dt.uint32
I32 = mybir.dt.int32
U8 = mybir.dt.uint8
FP8X4 = mybir.dt.float8_e4m3fn_x4
ACT = mybir.ActivationFunctionType
ALU = mybir.AluOpType

P = 128
TILES = V // P
CHUNK = 2
BLOCK = ((2, 3, 4), (0, 1, 5))


def tile_neuralblendshapelinearskinning_x2_kernel(
    tc, pose, w1_words, w1_scales, g, basis, template, skin_words, skin_scales, xf, out_0, out_1, out_2
):
    nc = tc.nc
    with ExitStack() as ctx:
        keep = ctx.enter_context(tc.tile_pool(name="keep", bufs=1))
        work = ctx.enter_context(tc.tile_pool(name="work", bufs=2))
        psum = ctx.enter_context(tc.psum_pool(name="psum", bufs=1))
        ctx.enter_context(tc.manual_schedule())

        def bank(tag, shape, dtype=F32):
            return psum.tile(shape, dtype, tag=tag, name=tag)

        def copy_on(engine, out, in_):
            if engine == "vector":
                nc.vector.tensor_copy(out=out, in_=in_)
            else:
                nc.scalar.copy(out=out, in_=in_)

        def quantize(codes, scales, values, spans):
            for lo, hi in spans:
                nc.vector.quantize_mx(
                    out=codes[:, lo:hi].bitcast(FP8X4), scales=scales[:, lo:hi], in_=values[:, 4 * lo : 4 * hi]
                )

        def mx(out, lhs, lhs_cols, rhs, rhs_cols, start=True, stop=True):
            nc.tensor.matmul_mx(
                out=out,
                lhsT=lhs[0][:, lhs_cols].bitcast(FP8X4),
                lhsT_scale=lhs[1][:, lhs_cols],
                rhs=rhs[0][:, rhs_cols].bitcast(FP8X4),
                rhs_scale=rhs[1][:, rhs_cols],
                start=start,
                stop=stop,
            )

        w1_c = keep.tile([P, H], U32, align_bytes=64)
        w1_s = keep.tile([P, H], U8, align_bytes=64)
        skin_c = keep.tile([P, V], U32, align_bytes=64)
        skin_s = keep.tile([P, V], U8, align_bytes=64)
        tmpl_rows = keep.tile([P, 3 * P], BF16)
        zero = keep.tile([P, 1], F32)
        zero_bias = keep.tile([P, 1], F32)
        nc.vector.memset(zero[:], 0.0)
        nc.vector.memset(w1_s[:].bitcast(I32), 0)
        nc.vector.memset(tmpl_rows[:], 0.0)
        nc.vector.memset(skin_s[:].bitcast(I32), 0)
        nc.scalar.activation(out=zero_bias[:], in_=zero[:], func=ACT.Tanh)
        ident = keep.tile([P, P], F32)
        ident_bf = keep.tile([P, P], BF16)
        make_identity(nc, ident[:])
        make_identity(nc, ident_bf[:])

        pose_sb = keep.tile([P, PD], BF16)
        xf_rows = xf.rearrange("(p t) b i k -> p t (b i k)", t=4)
        xf_raw = [keep.tile([P, 4, 768], BF16, name="xf_raw%d" % h) for h in range(2)]
        gain = keep.tile([P, 2, 4], BF16)
        basis_rows = basis.rearrange("(g p t) n c -> g p t (n c)", g=2, t=4)
        raw = {}

        def load_scales(plane, rows):
            for quad in range(4):
                nc.sync.dma_start(
                    out=plane[32 * quad : 32 * quad + 4, :].bitcast(I32),
                    in_=rows[0, 4 * quad : 4 * quad + 4, :].bitcast(I32),
                )

        def load_words(codes, words, lo, hi):
            nc.sync.dma_start(
                out=codes[:, lo:hi].bitcast(I32),
                in_=words[0].rearrange("p n t -> p (n t)")[:, 4 * lo : 4 * hi].bitcast(I32),
            )

        def load_basis(chunk, order=(1, 0)):
            first = CHUNK * chunk
            count = CHUNK
            for half in order:
                rows = keep.tile([P, 4, 384 * count], BF16, name="basis_raw%d_%d" % (chunk, half))
                nc.sync.dma_start(out=rows[:], in_=basis_rows[half, :, :, 384 * first : 384 * (first + count)])
                for q in range(count):
                    raw[first + q, half] = rows[:, :, 384 * q : 384 * (q + 1)]

        nc.sync.dma_start(out=pose_sb[:], in_=pose)
        nc.sync.dma_start(out=xf_raw[0][:], in_=xf_rows[:, :, 0:768])
        nc.sync.dma_start(out=gain[:], in_=g.rearrange("(g p t) -> p g t", g=2, t=4))
        load_scales(w1_s, w1_scales)
        nc.sync.dma_start(out=tmpl_rows[0:TILES, :], in_=template.rearrange("(q n) c -> q (n c)", n=P))
        nc.sync.dma_start(out=xf_raw[1][:], in_=xf_rows[:, :, 768:1536])
        load_words(w1_c, w1_words, 0, H)
        load_basis(0, (0, 1))
        load_scales(skin_s, skin_scales)
        load_words(skin_c, skin_words, 0, 256)
        load_basis(1)
        load_words(skin_c, skin_words, 256, 768)
        load_basis(2)
        load_words(skin_c, skin_words, 768, V)
        load_basis(3)

        pose_words = pose_sb[:].bitcast(F32)
        pose_t = bank("wa", [P, 2, P])
        for u in range(2):
            nc.tensor.transpose(pose_t[:, u, :], pose_words[:, u : 256 : 2], ident[:])
        pose_k = keep.tile([P, 4 * B], BF16, align_bytes=64)
        nc.scalar.copy(
            out=pose_k[:].bitcast(F32).rearrange("p (b u) -> p b u", u=2), in_=pose_t[:].rearrange("p u b -> p b u")
        )
        pose_q = (keep.tile([P, B], U32, align_bytes=64, name="pose_c"), keep.tile([P, B], U8, align_bytes=64, name="pose_s"))
        quantize(pose_q[0], pose_q[1], pose_k, [(0, B)])

        xf_k = keep.tile([P, 12 * B * 4], BF16, align_bytes=64)
        xf_k5 = xf_k[:].rearrange("p (i k b t) -> p i b t k", i=3, k=4, t=4)

        def interleave_xf(half, i, engine):
            src = xf_raw[half][:].rearrange("p t (b i k) -> p i b t k", i=3, k=4)
            copy_on(engine, xf_k5[:, i, 64 * half : 64 * half + 64], src[:, i])

        interleave_xf(0, 0, "vector")
        interleave_xf(0, 2, "scalar")
        interleave_xf(0, 1, "vector")
        interleave_xf(1, 0, "vector")

        interleave_xf(1, 2, "scalar")
        interleave_xf(1, 1, "vector")
        xf_q = (keep.tile([P, 12 * B], U32, align_bytes=64, name="xf_c"), keep.tile([P, 12 * B], U8, align_bytes=64, name="xf_s"))
        quantize(xf_q[0], xf_q[1], xf_k, [(1024, 1536), (0, 1024)])

        tanh_sb = keep.tile([P, 2, 4, P], F32)
        for half in range(2):
            pre = bank("v%d" % half, [P, 512])
            mx(pre[:], pose_q, slice(0, B), (w1_c, w1_s), slice(512 * half, 512 * half + 512))
            nc.scalar.activation(
                out=tanh_sb[:, half], in_=pre[:].rearrange("b (p t) -> b t p", t=4), func=ACT.Tanh, bias=zero_bias[:]
            )
        tmpl_t = bank("wb", [P, 3, P], BF16)
        for c in range(3):
            nc.tensor.transpose(tmpl_t[:, c, :], tmpl_rows[:, c : 3 * P : 3], ident_bf[:])
        tmpl = keep.tile([P, 3, TILES], F32)
        nc.scalar.copy(out=tmpl[:], in_=tmpl_t[:, :, 0:TILES])

        coef_k = keep.tile([P, 2, B, 4], BF16, align_bytes=64)
        for half in range(2):
            tanh_t = bank(("off", "m3")[half], [P, 4, B])
            for t in range(4):
                nc.tensor.transpose(tanh_t[:, t, :], tanh_sb[:, half, t, :], ident[:])
            nc.vector.tensor_tensor(
                out=coef_k[:, half],
                in0=tanh_t[:].rearrange("p t b -> p b t"),
                in1=gain[:, half, :].unsqueeze(1).to_broadcast([P, B, 4]),
                op=ALU.mult,
            )
        coef_q = (keep.tile([P, 2 * B], U32, align_bytes=64, name="coef_c"), keep.tile([P, 2 * B], U8, align_bytes=64, name="coef_s"))
        quantize(coef_q[0], coef_q[1], coef_k[:].rearrange("p g b t -> p (g b t)"), [(0, 2 * B)])

        basis_k, basis_q, off_ps, m3_ps, m_ps, u_sb, m3_sb, prod_sb, y_ps, y_bf, word_ps = ({} for k in range(11))
        skin_q = (skin_c, skin_s)

        basis_g = {}

        def main_tile(q):
            if q not in basis_k:
                basis_k[q] = work.tile([P, 5 * P * 4], BF16, align_bytes=64, bufs=3, name="basis_k")
            return basis_k[q]

        def interleave_low(q, lo, hi, engine):
            dst = main_tile(q)[:, 1024:2560].rearrange("p (c m l t) -> p m t l c", c=3, l=2, t=4)
            src = raw[q, 0].rearrange("p t (m l c) -> p m t l c", l=2, c=3)
            copy_on(engine, dst[:, lo // 2 : hi // 2], src[:, lo // 2 : hi // 2])

        def interleave_high(q, lo, hi, engine):
            dst = main_tile(q)[:, 0:1024].rearrange("p (c m l t) -> p m t l c", c=2, l=2, t=4)
            src = raw[q, 1].rearrange("p t (m l c) -> p m t l c", l=2, c=3)
            copy_on(engine, dst[:, lo // 2 : hi // 2], src[:, lo // 2 : hi // 2, :, :, 0:2])

        def interleave_rest(q, engine):
            basis_g[q] = keep.tile([P, P * 4], BF16, align_bytes=64, name="basis_first" if q == 0 else "basis_g")
            dst = basis_g[q][:].rearrange("p (n t) -> p n t", t=4)
            src = raw[q, 1].rearrange("p t (n c) -> p n t c", c=3)[:, :, :, 2]
            if engine == "gpsimd":
                nc.gpsimd.tensor_scalar(out=dst, in0=src, scalar1=1.0, scalar2=0.0, op0=ALU.mult, op1=ALU.add)
            else:
                copy_on(engine, dst, src)

        def interleave_scalar(q):
            interleave_high(q, 0, 64, "scalar")
            interleave_high(q, 64, 128, "scalar")

        def quantize_basis(q):
            codes = work.tile([P, 6 * P], U32, align_bytes=64, name="basis_c")
            scales = work.tile([P, 6 * P], U8, align_bytes=64, name="basis_s")
            basis_q[q] = (codes, scales)
            quantize(codes, scales, basis_k[q], [(0, 256), (256, 512), (512, 640)])
            quantize(codes[:, 640:768], scales[:, 640:768], basis_g[q], [(0, P)])

        def matmul_offsets(q):
            off_ps[q] = bank("off", [P, 3, B])
            for c in range(3):
                for half in range(2):
                    col = P * BLOCK[half][c]
                    mx(off_ps[q][:, c, :], basis_q[q], slice(col, col + P), coef_q, slice(B * half, B * half + B),
                       start=half == 0, stop=half == 1)
            m3_ps[q] = bank("m3", [P, 3, B])
            for i in range(3):
                mx(m3_ps[q][:, i, :], skin_q, slice(P * q, P * q + P), xf_q, slice(512 * i + 384, 512 * i + 512))

        def matmul_linear(q, tags=("v0", "v1", "v2")):
            for i in range(3):
                m_ps[q, i] = bank(tags[i], [P, 3 * B])
                mx(m_ps[q, i][:, 0:256], skin_q, slice(P * q, P * q + P), xf_q, slice(512 * i, 512 * i + 256))
                mx(m_ps[q, i][:, 256:384], skin_q, slice(P * q, P * q + P), xf_q, slice(512 * i + 256, 512 * i + 384))

        def shaped(q):
            u_sb[q] = work.tile([P, 3, B], F32, name="u_sb")
            for c in range(3):
                nc.scalar.activation(
                    out=u_sb[q][:, c, :], in_=off_ps[q][:, c, :], func=ACT.Identity, bias=tmpl[:, c, q : q + 1]
                )
            m3_sb[q] = work.tile([P, 3, B], F32, name="m3_sb")
            nc.scalar.copy(out=m3_sb[q][:], in_=m3_ps[q][:])

        def products(q):
            prod_sb[q] = work.tile([P, 3, 3 * B], F32, name="prod_sb")
            for i in range(3):
                nc.vector.tensor_tensor(
                    out=prod_sb[q][:, i, :], in0=m_ps[q, i][:], in1=u_sb[q][:].rearrange("p c b -> p (c b)"), op=ALU.mult
                )

        def accumulate(q):
            y_ps[q] = bank("off" if q == TILES - 1 else "y", [P, 3, P])
            for i in range(3):
                terms = [prod_sb[q][:, i, B * c : B * c + B] for c in range(3)] + [m3_sb[q][:, i, :]]
                for k in range(4):
                    nc.tensor.matmul(
                        y_ps[q][:, i, :], lhsT=terms[k], rhs=ident[:], start=k == 0, stop=k == 3, is_transpose=True
                    )

        def round_out(q):
            grp, r = divmod(q, 4)
            if r == 0:
                y_bf[grp] = work.tile([P, 3, 2, P, 2], BF16, name="y_bf")
            nc.scalar.copy(
                out=y_bf[grp][:, :, :, 32 * r : 32 * r + 32, :],
                in_=y_ps[q][:].rearrange("b i (p u e) -> b i u p e", u=2, e=2),
            )

        def hand_out(q):
            y_sb = work.tile([P, P, 3], F32, bufs=4)
            nc.scalar.copy(out=y_sb[:], in_=y_ps[q][:].rearrange("b i n -> b n i"))
            nc.sync.dma_start(out=out_0[:, P * q : P * q + P, :], in_=y_sb[:])

        def turn_words(grp, tags=("wa", "wb")):
            words = y_bf[grp][:].rearrange("b i u p e -> b (i u p e)").bitcast(F32)
            low = bank(tags[0], [P, 8, 64])
            high = bank(tags[1], [P, 8, 64])
            word_ps[grp] = (low, high)
            for j in range(6):
                nc.tensor.transpose(low[:, j : 8 : 7 - j, :], words[:, P * j : P * j + P], ident[:])
            for j in range(6):
                nc.tensor.transpose(high[:, 0 : j + 2 : j + 1, :], words[:, P * j : P * j + P], ident[:])

        plane_k = {}

        def gather_words(grp):
            plane_k[grp] = work.tile([P, 4 * 384], BF16, align_bytes=64, name="plane_k")
            dst = plane_k[grp][:].bitcast(F32).rearrange("p (b j) -> p b j", j=6)
            low, high = word_ps[grp]
            nc.scalar.copy(out=dst[:, 0:64, :], in_=low[:, 0:6, :].rearrange("p j b -> p b j"))
            copy_on("vector" if grp == 3 else "scalar", dst[:, 64:128, :], high[:, 1:7, :].rearrange("p j b -> p b j"))

        def store_planes(grp):
            plane_c = work.tile([P, 384], U32, align_bytes=64)
            plane_s = work.tile([P, 384], U8, align_bytes=64)
            quantize(plane_c, plane_s, plane_k[grp], [(0, 128), (128, 384)] if grp == 3 else [(0, 256), (256, 384)])
            nc.sync.dma_start(
                out=out_1[grp].rearrange("p m t -> p (m t)").bitcast(I32), in_=plane_c[:].bitcast(I32)
            )
            for quad in range(4):
                nc.sync.dma_start(
                    out=out_2[grp, 4 * quad : 4 * quad + 4, :].bitcast(I32),
                    in_=plane_s[32 * quad : 32 * quad + 4, :].bitcast(I32),
                )

        def live(q):
            return 0 <= q < TILES

        interleave_low(0, 0, 64, "scalar")
        interleave_low(0, 64, 128, "scalar")
        interleave_low(1, 0, 128, "vector")
        interleave_high(0, 0, 64, "scalar")
        interleave_high(0, 64, 128, "vector")
        interleave_rest(0, "vector")
        interleave_rest(1, "scalar")
        interleave_scalar(1)
        quantize_basis(0)
        matmul_offsets(0)
        shaped(0)
        matmul_linear(0)
        quantize_basis(1)
        interleave_scalar(2)
        last = TILES - 1
        for s in range(last - 1):
            matmul_offsets(s + 1)
            interleave_rest(s + 2, "gpsimd")
            products(s)
            if s > 0:
                round_out(s - 1)
                hand_out(s - 1)
            if s % 2 == 1 and live(s + 7):
                load_basis(4 + s // 2)
            if s + 2 == last:
                interleave_low(last, 96, 128, "scalar")
            shaped(s + 1)
            matmul_linear(s + 1)
            accumulate(s)
            if s > 0 and s % 4 == 0:
                turn_words(s // 4 - 1)
            if s > 1 and s % 4 == 1:
                gather_words(s // 4 - 1)
            if live(s + 3):
                interleave_scalar(s + 3)
            interleave_low(s + 2, 0, 96 if s + 2 == last else P, "vector")
            if s > 2 and s % 4 == 2:
                store_planes(s // 4 - 1)
            quantize_basis(s + 2)
        matmul_offsets(last)
        products(last - 1)
        round_out(last - 2)
        hand_out(last - 2)
        shaped(last)
        matmul_linear(last, ("wa", "wb", "v0"))
        products(last)
        store_planes(2)
        accumulate(last - 1)
        accumulate(last)
        round_out(last - 1)
        hand_out(last - 1)
        round_out(last)
        turn_words(3, ("v1", "v2"))
        hand_out(last)
        gather_words(3)
        store_planes(3)
